import numpy as np
import ml_dtypes


def mxq(x, axis, fmt="e4m3"):
    dtype, down = {"e4m3": (ml_dtypes.float8_e4m3fn, 7), "e5m2": (ml_dtypes.float8_e5m2, 14)}[fmt]
    v = np.moveaxis(np.asarray(x, np.float32).astype(ml_dtypes.bfloat16).astype(np.float64), axis, -1)
    blocks = v.reshape(v.shape[:-1] + (-1, 32))
    amax = np.abs(blocks).max(-1, keepdims=True)
    byte = np.maximum(np.where(amax > 0, np.frexp(amax)[1] - 1 + 127, 0) - down, 1)
    scale = np.exp2(byte - 127.0)
    codes = (blocks / scale).astype(np.float32).astype(dtype).astype(np.float64)
    return np.moveaxis((codes * scale).reshape(v.shape), -1, axis)


WIDE = False


def mx_kscale(k):
    if not WIDE:
        return np.ones(k)
    levels = np.array([10, -10, 5, -5, 0])
    if k % 512:
        return np.exp2(np.random.permutation(np.resize(levels, k // 32))).repeat(32)
    a = np.empty((k // 512, 16))
    for p in range(k // 512):
        a[p, :8] = np.random.permutation(np.resize(levels, 8))
        for g in range(8):
            far = levels[np.abs(levels - a[p, g]) >= 10]
            a[p, g + 8] = far[np.random.randint(len(far))]
    return np.exp2(a.ravel()).repeat(32)


BF16 = ml_dtypes.bfloat16


def bf(x):
    return np.asarray(x, np.float32).astype(BF16)


def f64(x):
    return np.asarray(x).astype(np.float64)


E2M1 = np.array([0.0, 0.5, 1.0, 1.5, 2.0, 3.0, 4.0, 6.0, -0.0, -0.5, -1.0, -1.5, -2.0, -3.0, -4.0, -6.0])


def pack_weight(w, fmt):
    k, n = w.shape
    w = f64(bf(w)).reshape(k // 32, 32, n)
    amax = np.abs(w).max(1)
    if fmt == "e4m3":
        byte = np.frexp(amax)[1] - 1 + 127 - 7
    else:
        mant, ex = np.frexp(amax / 6.0)
        byte = np.where(mant > 0.5, ex, ex - 1) + 127
    byte = np.clip(np.where(amax > 0, byte, 1), 1, 254)
    scaled = (w * np.exp2(127.0 - byte)[:, None, :]).reshape(k, n).astype(np.float32)
    by_word = np.ascontiguousarray(scaled.reshape(k // 512, 128, 4, n).transpose(0, 1, 3, 2))
    if fmt == "e4m3":
        words = by_word.astype(ml_dtypes.float8_e4m3fn).view(np.uint8)
    else:
        c = by_word.astype(ml_dtypes.float4_e2m1fn).view(np.uint8) & 0xF
        words = c[..., 0::2] | (c[..., 1::2] << 4)
    return np.ascontiguousarray(words), np.ascontiguousarray(byte.astype(np.uint8).reshape(k // 512, 16, n))


def unpack_weight(words, scales, fmt):
    g, p, n, _ = words.shape
    if fmt == "e4m3":
        vals = np.ascontiguousarray(words).view(ml_dtypes.float8_e4m3fn).astype(np.float64)
    else:
        nib = np.empty((g, p, n, 4), np.uint8)
        nib[..., 0::2] = words & 0xF
        nib[..., 1::2] = words >> 4
        vals = E2M1[nib]
    vals = vals * np.repeat(np.exp2(scales.astype(np.float64) - 127.0), 8, axis=1)[..., None]
    return vals.transpose(0, 1, 3, 2).reshape(g * 512, n)
def pack4(w):
    words, scales = pack_weight(w, "e2m1")
    return words.reshape(words.shape[0], 128, -1), scales


def unpack4(words, scales):
    return unpack_weight(words.reshape(words.shape[0], 128, -1, 2), scales, "e2m1")


def planes(Y):
    n, m = Y.shape
    b = f64(bf(Y)).reshape(n // 32, 32, m)
    amax = np.abs(b).max(1)
    byte = np.clip(np.where(amax > 0, np.frexp(amax)[1] - 1 + 127 - 7, 1), 1, 254)
    codes = (b * np.exp2(127.0 - byte)[:, None, :]).reshape(n, m).astype(np.float32).astype(ml_dtypes.float8_e4m3fn).view(np.uint8)
    words = codes.reshape(n // 512, 128, 4, m).transpose(0, 1, 3, 2)
    return np.ascontiguousarray(words), np.ascontiguousarray(byte.astype(np.uint8).reshape(n // 512, 16, m))


B, M, K, P = 512, 1024, 1024, 1024


def setup_inputs():
    a = mx_kscale(M)
    t = mx_kscale(K)
    u = bf(np.random.standard_normal((B, M)) * a)
    w_words, w_scales = pack4(np.random.standard_normal((M, K)) / np.sqrt(M) / a[:, None] * t[None, :])
    return {
        "u": u,
        "w_words": w_words,
        "w_scales": w_scales,
        "theta": bf(np.random.uniform(-3.14, 3.14, (P, K))),
        "fx": bf(np.random.standard_normal(K)),
        "ft": bf(np.random.standard_normal(K)),
        "nu": bf(np.random.uniform(0.1, 0.4, P)),
        "g": bf((1.0 + 0.1 * np.random.standard_normal(K)) / t),
    }


def _trunk_features(theta, fx, ft, nu, g):
    sn = np.sin(theta)
    cs = np.cos(theta)
    gain = g[None, :]
    fx_row = fx[None, :]
    ft_row = ft[None, :]
    nu_col = nu[:, None]
    t0 = gain * sn
    tx = gain * (fx_row * cs)
    tl = gain * (ft_row * cs + nu_col * fx_row * fx_row * sn)
    return t0, tx, tl


def _contract_modes(cq, t):
    return (cq @ mxq(t, 1, "e4m3").T) / np.sqrt(cq.shape[1])


def core(u, w_words, w_scales, theta, fx, ft, nu, g):
    c = mxq(f64(u), 1, "e4m3") @ unpack4(w_words, w_scales)
    t0, tx, tl = _trunk_features(f64(theta), f64(fx), f64(ft), f64(nu), f64(g))
    cq = mxq(c, 1, "e4m3")
    s = _contract_modes(cq, t0)
    sx = _contract_modes(cq, tx)
    sl = _contract_modes(cq, tl)
    r = sl + s * sx
    return r


def reference(u, w_words, w_scales, theta, fx, ft, nu, g):
    R_out = core(u, w_words, w_scales, theta, fx, ft, nu, g)
    words, scales = planes(R_out.T)
    return R_out, words, scales

import math
from contextlib import ExitStack

import concourse.mybir as mybir
from concourse.masks import make_identity

F32 = mybir.dt.float32
BF16 = mybir.dt.bfloat16
I32 = mybir.dt.int32
U32 = mybir.dt.uint32
U8 = mybir.dt.uint8
FP8X4 = mybir.dt.float8_e4m3fn_x4
FP4X4 = mybir.dt.float4_e2m1fn_x4
ALU = mybir.AluOpType
ACT = mybir.ActivationFunctionType

B, M, K, NP = 512, 1024, 1024, 1024
P = 128
PASS = 512
GROUPS = K // PASS
BT = B // P
FLOPS = 2 * B * M * K + 3 * 2 * B * K * NP

CHUNKS = [(0, 128), (128, 256), (384, 256), (640, 256), (896, 128)]
SHARE = {}
UNITS = [(c, grp) for c in range(len(CHUNKS)) for grp in range(GROUPS)]
EPIS = [(c, b0, PASS // CHUNKS[c][1]) for c in range(len(CHUNKS)) for b0 in range(0, BT, PASS // CHUNKS[c][1])]


def tile_pideeponetburgersresidual_x2_kernel(tc, u, w_words, w_scales, theta, fx, ft, nu, g, out_0, out_1, out_2):
    nc = tc.nc
    with ExitStack() as ctx:
        keep = ctx.enter_context(tc.tile_pool(name="keep", bufs=1))
        work = ctx.enter_context(tc.tile_pool(name="work", bufs=2))
        turn = ctx.enter_context(tc.psum_pool(name="turn", bufs=3))
        sums = ctx.enter_context(tc.psum_pool(name="sums", bufs=3))
        fixed = ctx.enter_context(tc.psum_pool(name="fixed", bufs=1))
        ctx.enter_context(tc.manual_schedule())

        ident32 = keep.tile([P, P], F32, name="ident32")
        ident16 = keep.tile([P, P], BF16, name="ident16")
        g_sb = keep.tile([P, GROUPS, 4], BF16, name="g_sb")
        fx_sb = keep.tile([P, GROUPS, 4], BF16, name="fx_sb")
        ft_sb = keep.tile([P, GROUPS, 4], BF16, name="ft_sb")
        nu_sb = keep.tile([P, 8], BF16, name="nu_sb")
        gains = keep.tile([P, P], F32, name="gains")
        gains_t = keep.tile([P, P], F32, name="gains_t")
        coef_cos = keep.tile([P, 8], F32, name="coef_cos")
        coef_sin = keep.tile([P, 8], F32, name="coef_sin")
        warm = keep.tile([P, 8], F32, name="warm")
        gains_ps = fixed.tile([P, P], F32, name="gains_ps")
        nu_ps = fixed.tile([P, 8, P], BF16, name="nu_ps")
        w_sb = keep.tile([P, GROUPS, 2 * K], U8, name="w_sb", align_bytes=64)
        ws_sb = keep.tile([P, GROUPS, K], U8, name="ws_sb", align_bytes=64)
        u_sb = [keep.tile([P, M], BF16, name="u_sb%d" % b) for b in range(BT)]
        ut = [keep.tile([P, 2, GROUPS, P, 4], BF16, name="ut%d" % h, align_bytes=64) for h in range(2)]
        uq = [keep.tile([P, 2, GROUPS, P], U32, name="uq%d" % h, align_bytes=64) for h in range(2)]
        us = [keep.tile([P, 2, GROUPS, P], U8, name="us%d" % h, align_bytes=64) for h in range(2)]
        c_sb = [keep.tile([P, GROUPS, PASS], BF16, name="c_sb%d" % b) for b in range(BT)]
        ct = [keep.tile([P, 2, GROUPS, P, 4], BF16, name="ct%d" % h, align_bytes=64) for h in range(2)]
        cq = [keep.tile([P, 2, GROUPS, P], U32, name="cq%d" % h, align_bytes=64) for h in range(2)]
        cs = [keep.tile([P, 2, GROUPS, P], U8, name="cs%d" % h, align_bytes=64) for h in range(2)]
        th = [keep.tile([P, CHUNKS[c][1] // P, PASS], BF16, name="th%d" % n) for n, (c, grp) in enumerate(UNITS)]
        fq = [keep.tile([P, GROUPS, 2, rows], U32, name="fq%d" % c, align_bytes=64) for c, (r0, rows) in enumerate(CHUNKS)]
        fs = [keep.tile([P, GROUPS, 2, rows], U8, name="fs%d" % c, align_bytes=64) for c, (r0, rows) in enumerate(CHUNKS)]
        lq = [keep.tile([P, GROUPS, rows], U32, name="lq%d" % c, align_bytes=64) for c, (r0, rows) in enumerate(CHUNKS)]
        ls = [keep.tile([P, GROUPS, rows], U8, name="ls%d" % c, align_bytes=64) for c, (r0, rows) in enumerate(CHUNKS)]
        r16 = keep.tile([P, BT, NP], BF16, name="r16")
        rt = [keep.tile([P, B, 4], BF16, name="rt%d" % h, align_bytes=64) for h in range(2)]
        rq = [keep.tile([P, B], U32, name="rq%d" % h, align_bytes=64) for h in range(2)]
        rs = [keep.tile([P, B], U8, name="rs%d" % h, align_bytes=64) for h in range(2)]
        live = {}

        def rows_of(n):
            return CHUNKS[UNITS[n][0]][1]

        def load_theta(n):
            c, grp = UNITS[n]
            r0, rows = CHUNKS[c]
            src = theta[r0 : r0 + rows, grp * PASS : (grp + 1) * PASS]
            nc.sync.dma_start(out=th[n][:], in_=src.rearrange("(j p) k -> p j k", p=P))

        def load_u(b):
            nc.sync.dma_start(out=u_sb[b][:], in_=u[b * P : (b + 1) * P, :])

        def load_w():
            nc.sync.dma_start(out=w_sb[:].bitcast(I32), in_=w_words.rearrange("g p n -> p g n").bitcast(I32))
            for q in range(4):
                src = w_scales[:, 4 * q : 4 * q + 4, :].rearrange("g r n -> r g n")
                nc.sync.dma_start(out=ws_sb[32 * q : 32 * q + 4, :, :].bitcast(I32), in_=src.bitcast(I32))

        def load_small():
            for dst, vec in ((g_sb, g), (fx_sb, fx), (ft_sb, ft)):
                nc.scalar.dma_start(out=dst[:], in_=vec.rearrange("(h p t) -> p h t", p=P, t=4))
            nc.scalar.dma_start(out=nu_sb[:], in_=nu.rearrange("(p j) -> p j", j=8))

        def make_constants():
            flat = "p h t -> p (h t)"
            g8, fx8, ft8 = g_sb[:].rearrange(flat), fx_sb[:].rearrange(flat), ft_sb[:].rearrange(flat)
            nc.vector.tensor_tensor(out=gains[:, 8:16], in0=g8, in1=fx8, op=ALU.mult)
            nc.vector.tensor_copy(out=gains[:, 0:8], in_=g8)
            nc.vector.tensor_tensor(out=coef_cos[:], in0=g8, in1=ft8, op=ALU.mult)
            nc.vector.tensor_tensor(out=coef_sin[:], in0=gains[:, 8:16], in1=fx8, op=ALU.mult)

        def gains_there():
            bank = turn.tile([P, P], F32, name="gains_bank", tag="turn")
            nc.tensor.transpose(bank[:], gains[:], ident32[:])
            live["gains_t"] = bank

        def gains_copy():
            nc.vector.tensor_copy(out=gains_t[:], in_=live["gains_t"][:])

        def gains_back():
            nc.tensor.transpose(gains_ps[:], gains_t[:], ident32[:])

        def spread_nu():
            for j in range(8):
                nc.tensor.transpose(nu_ps[:, j, :], nu_sb[:, j : j + 1].to_broadcast([P, P]), ident16[:])

        def abs_theta(n):
            nj = rows_of(n) // P
            mag = work.tile([P, nj, 2, P], F32, name="mag", tag="mag", bufs=4)
            src = th[n][:].bitcast(I32).rearrange("p j (q u) -> p j u q", u=2)
            nc.vector.tensor_scalar(out=mag[:].bitcast(I32), in0=src, scalar1=0x7FFF7FFF, scalar2=None, op0=ALU.bitwise_and)
            live["mag", n] = mag

        def turn_theta(n):
            nj = rows_of(n) // P
            bank = turn.tile([P, 2, nj, P], F32, name="theta_bank", tag="turn")
            for j in range(nj):
                words = th[n][:, j, :].bitcast(F32)
                for half in range(2):
                    nc.tensor.transpose(bank[:, half, j, :], words[:, half : 2 * P : 2], ident32[:])
            live["theta_t", n] = bank

        def turn_mag(n):
            nj = rows_of(n) // P
            bank = turn.tile([P, 2, nj, P], F32, name="mag_bank", tag="turn")
            for j in range(nj):
                for half in range(2):
                    nc.tensor.transpose(bank[:, half, j, :], live["mag", n][:, j, half, :], ident32[:])
            live["mag_t", n] = bank

        def angles(bank):
            return bank[:].rearrange("p u j r -> p u (j r)").bitcast(BF16).rearrange("p u (r e) -> p u e r", e=2)

        def sine(n):
            sin = work.tile([P, 4, rows_of(n)], F32, name="sin", tag="sin", bufs=3)
            nc.scalar.activation(out=sin[:].rearrange("p (u e) r -> p u e r", e=2), in_=angles(live["theta_t", n]), func=ACT.Sin)
            live["sin", n] = sin

        def cosine(n):
            cos = work.tile([P, 4, rows_of(n)], F32, name="cos", tag="cos", bufs=3)
            nc.scalar.activation(
                out=cos[:].rearrange("p (u e) r -> p u e r", e=2), in_=angles(live["mag_t", n]), func=ACT.Sin, scale=-1.0, bias=math.pi / 2
            )
            live["cos", n] = cos

        def cos_term(n):
            grp = UNITS[n][1]
            term = work.tile([P, rows_of(n) // 4, 4, 4], F32, name="cos_term", tag="cos_term", bufs=3)
            for t in range(4):
                src = live["cos", n][:, t, :].rearrange("p (c i) -> p c i", i=4)
                col = 4 * grp + t
                nc.scalar.activation(out=term[:, :, t, :], in_=src, func=ACT.Copy, scale=coef_cos[:, col : col + 1])
            live["cos_term", n] = term

        def sin_term(n):
            c, grp = UNITS[n]
            r0, rows = CHUNKS[c]
            term = work.tile([P, rows // 4, 4, 4], F32, name="sin_term", tag="sin_term", bufs=2)
            nu_rows = nu_ps[:, :, r0 // 8 : (r0 + rows) // 8].rearrange("p (h i) a -> p a h i", h=2)
            for t in range(4):
                col = 4 * grp + t
                nc.vector.scalar_tensor_tensor(
                    out=term[:, :, t, :].rearrange("p (a h) i -> p a h i", h=2),
                    in0=live["sin", n][:, t, :].rearrange("p (a h i) -> p a h i", h=2, i=4),
                    scalar=coef_sin[:, col : col + 1],
                    in1=nu_rows,
                    op0=ALU.mult,
                    op1=ALU.mult,
                )
            live["sin_term", n] = term

        def shared_rows(n):
            return SHARE.get(n, 0)

        def pair_tile(n):
            if ("pair", n) not in live:
                tag = "pair_first" if n == 0 else "pair"
                live["pair", n] = work.tile([P, 2, rows_of(n), 4], BF16, name="pair", tag=tag, bufs=1, align_bytes=64)
            return live["pair", n]

        def scaled(n, f):
            grp = UNITS[n][1]
            rows = rows_of(n)
            lo = shared_rows(n) if f == 0 else 0
            col = 8 * f + 4 * grp
            source = gains if n == 0 else gains_ps
            gain = source[:, col : col + 4].unsqueeze(1).unsqueeze(3).to_broadcast([P, (rows - lo) // 2, 4, 2])
            nc.vector.tensor_tensor(
                out=pair_tile(n)[:, f, lo:rows, :].rearrange("p (c i) t -> p c t i", i=2),
                in0=live["cos" if f else "sin", n][:, :, lo:rows].rearrange("p t (c i) -> p c t i", i=2),
                in1=gain,
                op=ALU.mult,
            )

        def share(n):
            grp = UNITS[n][1]
            lo = shared_rows(n)
            gain = gains[:, 4 * grp : 4 * grp + 4].unsqueeze(1).unsqueeze(3).to_broadcast([P, lo // 4, 4, 4])
            nc.gpsimd.tensor_tensor(
                out=pair_tile(n)[:, 0, 0:lo, :].rearrange("p (c i) t -> p c t i", i=4),
                in0=live["sin", n][:, :, 0:lo].rearrange("p t (c i) -> p c t i", i=4),
                in1=gain,
                op=ALU.mult,
            )

        def add_terms(n, on):
            engine = nc.vector if on == "vector" else nc.gpsimd
            tl = work.tile([P, rows_of(n), 4], BF16, name="tl", tag="tl", bufs=2, align_bytes=64)
            engine.tensor_tensor(
                out=tl[:].rearrange("p (c i) t -> p c t i", i=4), in0=live["sin_term", n][:], in1=live["cos_term", n][:], op=ALU.add
            )
            live["tl", n] = tl

        def quantize_pair(n):
            c, grp = UNITS[n]
            nc.vector.quantize_mx(
                out=fq[c][:, grp, :, :].rearrange("p f r -> p (f r)").bitcast(FP8X4),
                scales=fs[c][:, grp, :, :].rearrange("p f r -> p (f r)"),
                in_=live["pair", n][:].rearrange("p f r t -> p (f r t)"),
            )

        def quantize_tl(n):
            c, grp = UNITS[n]
            nc.vector.quantize_mx(
                out=lq[c][:, grp, :].bitcast(FP8X4), scales=ls[c][:, grp, :], in_=live["tl", n][:].rearrange("p r t -> p (r t)")
            )

        def turn_u(b):
            bank = turn.tile([P, GROUPS, 2, P], F32, name="u_bank", tag="turn")
            words = u_sb[b][:].bitcast(F32)
            for grp in range(GROUPS):
                for half in range(2):
                    nc.tensor.transpose(bank[:, grp, half, :], words[:, 256 * grp + half : 256 * (grp + 1) : 2], ident32[:])
            live["u_t", b] = bank

        def copy_words(engine, dst, bank):
            src = bank[:].rearrange("p a u r -> p a r u")
            if engine == "scalar":
                nc.scalar.copy(out=dst.bitcast(F32), in_=src)
            else:
                nc.vector.tensor_copy(out=dst.bitcast(F32), in_=src)

        def copy_u(b, engine):
            copy_words(engine, ut[b // 2][:, b % 2, :, :, :], live["u_t", b])

        def quantize_rows(codes, scales, values):
            nc.vector.quantize_mx(
                out=codes[:].rearrange("p a g r -> p (a g r)").bitcast(FP8X4),
                scales=scales[:].rearrange("p a g r -> p (a g r)"),
                in_=values[:].rearrange("p a g r t -> p (a g r t)"),
            )

        def branch(b, h):
            acc = sums.tile([P, PASS], F32, name="c_acc", tag="sums")
            for grp in range(GROUPS):
                nc.tensor.matmul_mx(
                    out=acc[:],
                    lhsT=uq[b // 2][:, b % 2, grp, :].bitcast(FP8X4),
                    lhsT_scale=us[b // 2][:, b % 2, grp, :],
                    rhs=w_sb[:, grp, 2 * PASS * h : 2 * PASS * (h + 1)].bitcast(FP4X4),
                    rhs_scale=ws_sb[:, grp, PASS * h : PASS * (h + 1)],
                    start=grp == 0,
                    stop=grp == GROUPS - 1,
                )
            live["c_acc", b, h] = acc

        def round_c(b, h, engine):
            dst = c_sb[b][:, h, :].rearrange("p (u q e) -> p u q e", u=2, e=2)
            src = live["c_acc", b, h][:].rearrange("p (q u e) -> p u q e", u=2, e=2)
            if engine == "scalar":
                nc.scalar.copy(out=dst, in_=src)
            else:
                nc.vector.tensor_copy(out=dst, in_=src)

        def turn_c(b):
            bank = turn.tile([P, GROUPS, 2, P], F32, name="c_bank", tag="turn")
            for h in range(GROUPS):
                words = c_sb[b][:, h, :].bitcast(F32)
                for half in range(2):
                    nc.tensor.transpose(bank[:, h, half, :], words[:, P * half : P * (half + 1)], ident32[:])
            live["c_t", b] = bank

        def copy_c(b, engine):
            copy_words(engine, ct[b // 2][:, b % 2, :, :, :], live["c_t", b])

        def contract(e, f):
            c, b0, nb = EPIS[e]
            rows = CHUNKS[c][1]
            acc = sums.tile([P, nb, rows], F32, name="acc", tag="sums")
            for a in range(nb):
                b = b0 + a
                for grp in range(GROUPS):
                    codes = lq[c][:, grp, :] if f == 2 else fq[c][:, grp, f, :]
                    scales = ls[c][:, grp, :] if f == 2 else fs[c][:, grp, f, :]
                    nc.tensor.matmul_mx(
                        out=acc[:, a, :],
                        lhsT=cq[b // 2][:, b % 2, grp, :].bitcast(FP8X4),
                        lhsT_scale=cs[b // 2][:, b % 2, grp, :],
                        rhs=codes.bitcast(FP8X4),
                        rhs_scale=scales,
                        start=grp == 0,
                        stop=grp == GROUPS - 1,
                    )
            live["acc", e, f] = acc

        def scale_s(e):
            c, b0, nb = EPIS[e]
            s_sb = work.tile([P, nb, CHUNKS[c][1]], F32, name="s_sb", tag="s_sb", bufs=2)
            nc.scalar.activation(out=s_sb[:], in_=live["acc", e, 0][:], func=ACT.Copy, scale=1.0 / K)
            live["s", e] = s_sb

        def product(e):
            c, b0, nb = EPIS[e]
            prod = work.tile([P, nb, CHUNKS[c][1]], F32, name="prod", tag="prod", bufs=2)
            nc.vector.tensor_tensor(out=prod[:], in0=live["s", e][:], in1=live["acc", e, 1][:], op=ALU.mult)
            live["prod", e] = prod

        def residual_into(e, dst, tiles):
            nc.vector.scalar_tensor_tensor(
                out=dst,
                in0=live["acc", e, 2][:, tiles, :],
                scalar=1.0 / math.sqrt(K),
                in1=live["prod", e][:, tiles, :],
                op0=ALU.mult,
                op1=ALU.add,
            )

        def r16_part(e):
            c, b0, nb = EPIS[e]
            r0, rows = CHUNKS[c]
            return r16[:, b0 : b0 + nb, r0 : r0 + rows]

        def residual(e):
            c, b0, nb = EPIS[e]
            r0, rows = CHUNKS[c]
            r32 = work.tile([P, nb, rows], F32, name="r32", tag="r32", bufs=3)
            residual_into(e, r32[:], slice(0, nb))
            dst = out_0[b0 * P : (b0 + nb) * P, r0 : r0 + rows].rearrange("(a p) r -> p a r", p=P)
            nc.sync.dma_start(out=dst, in_=r32[:])
            live["r32", e] = r32

        def round_r(e, engine):
            if engine == "scalar":
                nc.scalar.copy(out=r16_part(e), in_=live["r32", e][:])
            else:
                nc.gpsimd.tensor_scalar(out=r16_part(e), in0=live["r32", e][:], scalar1=1.0, scalar2=1.0, op0=ALU.mult, op1=ALU.mult)

        def turn_r(h, pair):
            bank = turn.tile([P, 2, 2, P], F32, name="r_bank", tag="turn")
            for a in range(2):
                words = r16[:, 2 * pair + a, PASS * h : PASS * (h + 1)].bitcast(F32)
                for half in range(2):
                    nc.tensor.transpose(bank[:, a, half, :], words[:, half : 2 * P : 2], ident32[:])
            live["r_t", h, pair] = bank

        def copy_r(h, pair, engine):
            dst = rt[h][:, 2 * P * pair : 2 * P * (pair + 1), :].rearrange("p (a r) t -> p a r t", a=2)
            copy_words(engine, dst, live["r_t", h, pair])

        def quantize_r(h, cols):
            nc.vector.quantize_mx(
                out=rq[h][:, cols].bitcast(FP8X4), scales=rs[h][:, cols], in_=rt[h][:, cols, :].rearrange("p m t -> p (m t)")
            )
            dst = out_1[h, :, cols, :].rearrange("p m t -> p (m t)").bitcast(I32)
            nc.sync.dma_start(out=dst, in_=rq[h][:, cols].bitcast(I32))

        def store_scales(h, queues):
            for q in range(4):
                queues[q].dma_start(out=out_2[h, 4 * q : 4 * q + 4, :].bitcast(I32), in_=rs[h][32 * q : 32 * q + 4, :].bitcast(I32))

        def quantize_u(h):
            quantize_rows(uq[h], us[h], ut[h])

        def quantize_c(h):
            quantize_rows(cq[h], cs[h], ct[h])

        def planes_low():
            quantize_r(0, slice(0, B))
            store_scales(0, [nc.sync] * 4)

        def residual16(e, pair):
            tiles = slice(2 * pair, 2 * pair + 2)
            residual_into(e, r16_part(e)[:, tiles, :], tiles)

        def planes_high(pair):
            quantize_r(1, slice(2 * P * pair, 2 * P * (pair + 1)))
            if pair == 1:
                store_scales(1, [nc.sync, nc.scalar, nc.sync, nc.scalar])

        last = len(UNITS) - 1
        final = len(EPIS) - 1
        V, S, G = "vector", "scalar", "gpsimd"

        def needs(step):
            fn, a = step[0], step[1:]
            if fn is turn_mag:
                return [(abs_theta, a[0])]
            if fn is sine:
                return [(turn_theta, a[0])]
            if fn is cosine:
                return [(turn_mag, a[0])]
            if fn is cos_term:
                return [(cosine, a[0]), (make_constants,)]
            if fn is sin_term:
                return [(sine, a[0]), (spread_nu,), (make_constants,)]
            if fn is scaled:
                return [(cosine if a[1] else sine, a[0]), (gains_back,) if a[0] else (make_constants,)]
            if fn is share:
                return [(sine, a[0]), (quantize_pair, a[0] - 1)]
            if fn is quantize_pair:
                return [(scaled, a[0], 0), (scaled, a[0], 1)] + ([(share, a[0])] if shared_rows(a[0]) else [])
            if fn is add_terms:
                return [(sin_term, a[0]), (cos_term, a[0])]
            if fn is quantize_tl:
                return [(add_terms, a[0])]
            if fn is gains_there:
                return [(make_constants,)]
            if fn is gains_copy:
                return [(gains_there,)]
            if fn is gains_back:
                return [(gains_copy,)]
            if fn is copy_u:
                return [(turn_u, a[0])]
            if fn is quantize_u:
                return [(copy_u, 2 * a[0]), (copy_u, 2 * a[0] + 1)]
            if fn is branch:
                return [(quantize_u, a[0] // 2)]
            if fn is round_c:
                return [(branch, a[0], a[1])]
            if fn is turn_c:
                return [(round_c, a[0], 0), (round_c, a[0], 1)]
            if fn is copy_c:
                return [(turn_c, a[0])]
            if fn is quantize_c:
                return [(copy_c, 2 * a[0]), (copy_c, 2 * a[0] + 1)]
            if fn is contract:
                c, b0, nb = EPIS[a[0]]
                made = quantize_tl if a[1] == 2 else quantize_pair
                return [(made, 2 * c), (made, 2 * c + 1)] + [(quantize_c, b // 2) for b in range(b0, b0 + nb)]
            if fn is scale_s:
                return [(contract, a[0], 0)]
            if fn is product:
                return [(scale_s, a[0]), (contract, a[0], 1)]
            if fn is residual or fn is residual16:
                return [(product, a[0]), (contract, a[0], 2)]
            if fn is round_r:
                return [(residual, a[0])]
            if fn is turn_r:
                if a[0] == 0:
                    return [(round_r, e) for e in range(5)]
                return [(round_r, e) for e in range(final)] + [(residual16, final, a[1])]
            if fn is copy_r:
                return [(turn_r, a[0], a[1])]
            if fn is planes_low:
                return [(copy_r, 0, 0), (copy_r, 0, 1)]
            if fn is planes_high:
                return [(copy_r, 1, a[0])] + [(planes_high, 0)] * a[0]
            return []

        tensor_q = [
            (turn_theta, 0), (gains_there,), (turn_mag, 0), (spread_nu,), (turn_mag, 1), (gains_back,), (turn_theta, 1),
            (turn_theta, 2), (turn_mag, 2), (turn_u, 0), (turn_u, 1), (turn_u, 2), (turn_theta, 3), (turn_u, 3), (turn_mag, 3),
            (turn_theta, 4), (branch, 0, 0), (turn_mag, 4), (branch, 0, 1), (branch, 1, 0), (branch, 1, 1), (turn_c, 0),
            (branch, 2, 0), (branch, 3, 1), (branch, 2, 1), (branch, 3, 0), (turn_c, 1), (turn_c, 2), (turn_theta, 5), (turn_c, 3),
            (turn_mag, 5), (contract, 0, 0), (turn_mag, 6), (contract, 0, 1), (contract, 0, 2), (contract, 1, 0), (turn_theta, 6),
            (contract, 1, 1), (contract, 1, 2), (turn_theta, 7), (contract, 2, 0), (contract, 3, 0), (turn_mag, 7), (contract, 3, 1),
            (contract, 2, 1), (turn_mag, 9), (contract, 3, 2), (turn_theta, 8), (contract, 2, 2), (contract, 4, 1), (contract, 4, 0),
            (turn_theta, 9), (contract, 4, 2), (turn_mag, 8), (contract, 5, 0), (contract, 6, 0), (contract, 5, 1), (turn_r, 0, 1),
            (contract, 5, 2), (turn_r, 0, 0), (contract, 6, 1), (contract, 6, 2), (contract, 7, 0), (contract, 7, 1), (contract, 7, 2),
            (turn_r, 1, 0), (turn_r, 1, 1),
        ]
        scalar_q = [
            (sine, 0), (cosine, 0), (cos_term, 0), (cosine, 1), (sine, 1), (cos_term, 1), (sine, 2), (cosine, 2), (copy_u, 0, S),
            (cos_term, 2), (copy_u, 1, S), (copy_u, 2, S), (sine, 3), (cosine, 3), (sine, 4), (cos_term, 3), (cosine, 4),
            (round_c, 0, 1, S), (round_c, 1, 0, S), (cos_term, 4), (round_c, 1, 1, S), (round_c, 2, 0, S), (copy_c, 0, S),
            (round_c, 2, 1, S), (round_c, 3, 0, S), (round_c, 3, 1, S), (copy_c, 1, S), (copy_c, 3, S), (sine, 5), (cosine, 5),
            (scale_s, 0), (cos_term, 5), (cosine, 6), (sine, 6), (scale_s, 1), (cos_term, 6), (scale_s, 2), (scale_s, 3), (sine, 7),
            (round_r, 0, S), (sine, 8), (cosine, 7), (cos_term, 7), (cosine, 9), (round_r, 1, S), (scale_s, 4), (sine, 9),
            (cos_term, 9), (round_r, 3, S), (cosine, 8), (cos_term, 8), (round_r, 4, S), (scale_s, 5), (scale_s, 6), (copy_r, 0, 0, S),
            (scale_s, 7), (round_r, 5, S), (copy_r, 0, 1, S), (copy_r, 1, 0, S),
        ]
        vector_q = [
            (abs_theta, 0), (make_constants,), (gains_copy,), (abs_theta, 2), (abs_theta, 1), (scaled, 0, 0), (scaled, 0, 1),
            (quantize_pair, 0), (sin_term, 0), (sin_term, 1), (scaled, 1, 1), (scaled, 1, 0), (sin_term, 2), (abs_theta, 3),
            (abs_theta, 4), (quantize_pair, 1), (quantize_tl, 0), (quantize_tl, 1), (scaled, 2, 0), (scaled, 2, 1), (copy_u, 3, V),
            (quantize_u, 0), (quantize_u, 1), (quantize_tl, 2), (quantize_pair, 2), (sin_term, 3), (round_c, 0, 0, V), (scaled, 3, 0),
            (scaled, 3, 1), (abs_theta, 5), (quantize_pair, 3), (abs_theta, 6), (quantize_tl, 3), (sin_term, 4), (scaled, 4, 0),
            (copy_c, 2, V), (scaled, 4, 1), (quantize_c, 0), (quantize_c, 1), (abs_theta, 7), (quantize_tl, 4), (quantize_pair, 4),
            (sin_term, 5), (scaled, 5, 1), (product, 0), (scaled, 5, 0), (residual, 0), (quantize_pair, 5), (abs_theta, 9),
            (product, 1), (quantize_tl, 5), (residual, 1), (scaled, 6, 0), (sin_term, 6), (product, 3), (scaled, 6, 1), (product, 2),
            (residual, 3), (abs_theta, 8), (quantize_pair, 6), (residual, 2), (sin_term, 7), (quantize_tl, 6), (scaled, 7, 1),
            (scaled, 7, 0), (product, 4), (quantize_pair, 7), (residual, 4), (scaled, 8, 1), (sin_term, 8), (quantize_tl, 7),
            (sin_term, 9), (scaled, 8, 0), (product, 5), (quantize_pair, 8), (add_terms, 9, V), (scaled, 9, 1), (scaled, 9, 0),
            (residual, 5), (quantize_pair, 9), (product, 6), (quantize_tl, 9), (quantize_tl, 8), (residual, 6), (product, 7),
            (residual16, 7, 0), (residual16, 7, 1), (residual, 7), (planes_low,), (copy_r, 1, 1, V), (planes_high, 0),
            (planes_high, 1),
        ]
        pool_q = [
            (add_terms, 0, G), (add_terms, 1, G), (add_terms, 2, G), (add_terms, 3, G), (add_terms, 4, G), (add_terms, 5, G),
            (add_terms, 6, G), (round_r, 2, G), (add_terms, 7, G), (add_terms, 8, G), (round_r, 6, G),
        ]

        load_small()
        load_theta(0)
        make_identity(nc, ident16[:])
        make_identity(nc, ident32[:])
        nc.vector.memset(warm[:], 0.0)
        nc.vector.memset(gains[:], 0.0)
        nc.vector.memset(ws_sb[:].bitcast(I32), 0)
        nc.scalar.activation(out=warm[:, 0:1], in_=warm[:, 1:2], func=ACT.Sin)
        load_theta(1)
        load_theta(2)
        for b in range(BT):
            load_u(b)
        load_theta(3)
        load_w()
        for n in range(4, len(UNITS)):
            load_theta(n)

        done = set()
        queues = [tensor_q, scalar_q, vector_q, pool_q]
        for sweep in range(sum(len(q) for q in queues)):
            for q in queues:
                if q and all(d in done for d in needs(q[0])):
                    step = q[0]
                    q.remove(step)
                    step[0](*step[1:])
                    done.add(tuple(x for x in step if x not in (V, S, G)))
        assert not any(queues)
